import numpy as np
import ml_dtypes


def mxq(x, axis, fmt="e4m3"):
    dtype, down = {"e4m3": (ml_dtypes.float8_e4m3fn, 7), "e5m2": (ml_dtypes.float8_e5m2, 14)}[fmt]
    v = np.moveaxis(np.asarray(x, np.float32).astype(ml_dtypes.bfloat16).astype(np.float64), axis, -1)
    blocks = v.reshape(v.shape[:-1] + (-1, 32))
    amax = np.abs(blocks).max(-1, keepdims=True)
    byte = np.maximum(np.where(amax > 0, np.frexp(amax)[1] - 1 + 127, 0) - down, 1)
    scale = np.exp2(byte - 127.0)
    codes = (blocks / scale).astype(np.float32).astype(dtype).astype(np.float64)
    return np.moveaxis((codes * scale).reshape(v.shape), -1, axis)


WIDE = False


def mx_kscale(k):
    if not WIDE:
        return np.ones(k)
    levels = np.array([10, -10, 5, -5, 0])
    if k % 512:
        return np.exp2(np.random.permutation(np.resize(levels, k // 32))).repeat(32)
    a = np.empty((k // 512, 16))
    for p in range(k // 512):
        a[p, :8] = np.random.permutation(np.resize(levels, 8))
        for g in range(8):
            far = levels[np.abs(levels - a[p, g]) >= 10]
            a[p, g + 8] = far[np.random.randint(len(far))]
    return np.exp2(a.ravel()).repeat(32)


def f64(x):
    return np.asarray(x).astype(np.float64)


def striped(idx):
    return np.tile(idx.reshape(-1, 16).T, (8, 1)).astype(np.uint16)


def unstriped(offs):
    return offs[:16].T.reshape(-1).astype(np.int64)


E2M1 = np.array([0.0, 0.5, 1.0, 1.5, 2.0, 3.0, 4.0, 6.0, -0.0, -0.5, -1.0, -1.5, -2.0, -3.0, -4.0, -6.0])


def pack_weight(w, fmt):
    k, n = w.shape
    w = f64(np.asarray(w, np.float32).astype(ml_dtypes.bfloat16)).reshape(k // 32, 32, n)
    amax = np.abs(w).max(1)
    if fmt == "e4m3":
        byte = np.frexp(amax)[1] - 1 + 127 - 7
    else:
        mant, ex = np.frexp(amax / 6.0)
        byte = np.where(mant > 0.5, ex, ex - 1) + 127
    byte = np.clip(np.where(amax > 0, byte, 1), 1, 254)
    scaled = (w * np.exp2(127.0 - byte)[:, None, :]).reshape(k, n).astype(np.float32)
    by_word = np.ascontiguousarray(scaled.reshape(k // 512, 128, 4, n).transpose(0, 1, 3, 2))
    if fmt == "e4m3":
        words = by_word.astype(ml_dtypes.float8_e4m3fn).view(np.uint8)
    else:
        c = by_word.astype(ml_dtypes.float4_e2m1fn).view(np.uint8) & 0xF
        words = (c[..., 0::2] | (c[..., 1::2] << 4)).reshape(k // 512, 128, 2 * n)
    return np.ascontiguousarray(words), np.ascontiguousarray(byte.astype(np.uint8).reshape(k // 512, 16, n))


def unpack_weight(words, scales, fmt):
    g, _, n = scales.shape
    words = np.ascontiguousarray(words).reshape(g, 128, n, -1)
    if fmt == "e4m3":
        vals = words.view(ml_dtypes.float8_e4m3fn).astype(np.float64)
    else:
        nib = np.empty((g, 128, n, 4), np.uint8)
        nib[..., 0::2] = words & 0xF
        nib[..., 1::2] = words >> 4
        vals = E2M1[nib]
    vals = vals * np.repeat(np.exp2(scales.astype(np.float64) - 127.0), 8, axis=1)[..., None]
    return vals.transpose(0, 1, 3, 2).reshape(g * 512, n)


def gelu(v):
    return 0.5 * v * (1.0 + np.tanh(np.sqrt(2.0 / np.pi) * (v + 0.044715 * v**3)))


K, M, H, N, T, S, P, L = 512, 1024, 512, 768, 2048, 1024, 512, 2048

def setup_inputs():
    n = np.random.standard_normal
    s = mx_kscale(K)[:, None]
    s2 = mx_kscale(M)[:, None]
    u = mx_kscale(H)[:, None]
    tab_words, tab_scales = pack_weight(n((K, T)) * s, "e4m3")
    tab2_words, tab2_scales = pack_weight(n((M, T)) * s2, "e4m3")
    w3_words, w3_scales = pack_weight(n((H, N)) / np.sqrt(H) / u, "e2m1")
    w5_words, w5_scales = pack_weight(n((M, N)) / np.sqrt(M) / s2, "e4m3")
    perm = np.random.permutation(L)
    return {
        "tab_words": tab_words, "tab_scales": tab_scales,
        "tab2_words": tab2_words, "tab2_scales": tab2_scales,
        "offs": striped(np.random.permutation(T)[:S]),
        "offs2": striped(np.random.permutation(T)[:P]),
        "pos1": striped(np.random.permutation(S)[:P]),
        "offs3": striped(perm[:S]),
        "offs4": striped(perm[S:S + P]),
        "w1": (0.8 * n((K, H)) / np.sqrt(K) / s * u.T).astype(np.float32),
        "w2": (0.55 * n((M, H)) / np.sqrt(M) / s2).astype(np.float32),
        "gain": (2.4 * np.exp(0.3 * n(H)) * u[:, 0]).astype(np.float32),
        "w3_words": w3_words, "w3_scales": w3_scales,
        "w4": (n((H, N)) / np.sqrt(H) / u).astype(np.float32),
        "w5_words": w5_words, "w5_scales": w5_scales,
        "page1": (0.6 * n((N, L))).astype(np.float32),
        "wg1": np.exp(0.3 * n((128, S))).astype(np.float32),
        "wg2": np.exp(0.3 * n((128, P))).astype(np.float32),
    }

def reference(tab_words, tab_scales, tab2_words, tab2_scales, offs, offs2, pos1, offs3, offs4, w1, w2, gain, w3_words, w3_scales, w4, w5_words, w5_scales, page1, wg1, wg2):
    v = unpack_weight(tab_words, tab_scales, "e4m3")[:, unstriped(offs)]
    v2 = unpack_weight(tab2_words, tab2_scales, "e4m3")[:, unstriped(offs2)]
    h1 = mxq(f64(w1), 0, "e4m3").T @ v
    h2 = mxq(f64(w2), 0, "e4m3").T @ v2
    z1 = np.abs(h1)
    z2 = np.sin(h2) * f64(gain)[:, None] - h1[:, unstriped(pos1)]
    y1 = unpack_weight(w3_words, w3_scales, "e2m1").T @ mxq(z1, 0, "e4m3")
    y2a = mxq(f64(w4), 0, "e4m3").T @ mxq(z2, 0, "e4m3")
    y2b = unpack_weight(w5_words, w5_scales, "e4m3").T @ v2
    y2 = np.maximum(y2a, y2b)
    out = f64(page1).copy()
    out[:, unstriped(offs3)] = np.tile(f64(wg1), (N // 128, 1)) * y1
    out[:, unstriped(offs4)] = np.tile(f64(wg2), (N // 128, 1)) * y2
    return out

@@ -1,0 +1,342 @@
+import math
+from contextlib import ExitStack
+
+import concourse.mybir as mybir
+from concourse.masks import make_identity
+
+K, M, H, N, T, S, PM, L = 512, 1024, 512, 768, 2048, 1024, 512, 2048
+FLOPS = 2 * (K * H * S + M * H * PM + H * N * S + H * N * PM + M * N * PM)
+
+F32 = mybir.dt.float32
+BF16 = mybir.dt.bfloat16
+I32 = mybir.dt.int32
+U32 = mybir.dt.uint32
+U16 = mybir.dt.uint16
+U8 = mybir.dt.uint8
+E4M3 = mybir.dt.float8_e4m3fn_x4
+E2M1 = mybir.dt.float4_e2m1fn_x4
+ACT = mybir.ActivationFunctionType
+ALU = mybir.AluOpType
+
+P = 128
+PACK = 4
+BANK = 512
+N_TILES = N // P
+ROUNDER = 1.5 * 2.0**23
+
+
+def tile_list_fraud_review_page_kernel(
+    tc, tab_words, tab_scales, tab2_words, tab2_scales, offs, offs2, pos1, offs3, offs4,
+    w1, w2, gain, w3_words, w3_scales, w4, w5_words, w5_scales, page1, wg1, wg2, out,
+):
+    nc = tc.nc
+    with ExitStack() as ctx:
+        lists = ctx.enter_context(tc.tile_pool(name="lists", bufs=1))
+        sb = ctx.enter_context(tc.tile_pool(name="sb", bufs=1))
+        ring = ctx.enter_context(tc.tile_pool(name="ring", bufs=3))
+        ps_a = ctx.enter_context(tc.psum_pool(name="ps_a", bufs=4))
+        ps_b = ctx.enter_context(tc.psum_pool(name="ps_b", bufs=4))
+
+        def held(shape, dtype, name, tag=None):
+            return sb.tile(shape, dtype, name=name, tag=tag or name, align_bytes=64)
+
+        def load_list(src, name):
+            t = lists.tile(list(src.shape), U16, name=name)
+            nc.sync.dma_start(t[:], src)
+            return t
+
+        def load_words(src, name, tag=None):
+            t = held([P, src.shape[1]], I32, name, tag)
+            nc.sync.dma_start(t[:], src.rearrange("p c i -> p (c i)").bitcast(I32))
+            return t
+
+        def load_scales(src, name, zero_engine, queue):
+            passes, width = src.shape[0], src.shape[2]
+            t = held([P, width], U8, name)
+            zero_engine.memset(t[:].bitcast(I32), 0)
+            for q in range(4):
+                queue.dma_start(
+                    t[32 * q : 32 * q + 4 * passes, :].bitcast(I32),
+                    src[:, 4 * q : 4 * q + 4, :].bitcast(I32),
+                )
+            return t
+
+        def load_rows(rows, name, tag=None):
+            t = held([P, PACK, rows.shape[1]], F32, name, tag)
+            nc.sync.dma_start(t[:], rows.rearrange("(p i) c -> p i c", i=PACK))
+            return t
+
+        def load_page(n, tag=None):
+            t = held([P, L], F32, "page%d" % n, tag)
+            nc.sync.dma_start(t[:], page1[P * n : P * (n + 1), :])
+            return t
+
+        def interleave(dst, src):
+            nc.scalar.copy(
+                dst.rearrange("p (c e) i -> p c i e", e=4),
+                src.rearrange("p i (c e) -> p c i e", e=4),
+            )
+
+        def quantize(src, name):
+            width = src.shape[1]
+            codes = held([P, width], U32, name + "_codes")
+            scales = held([P, width], U8, name + "_scales")
+            nc.vector.quantize_mx(
+                out=codes[:].bitcast(E4M3), scales=scales[:], in_=src.rearrange("p c i -> p (c i)")
+            )
+            return codes, scales
+
+        offs_t = load_list(offs, "offs_t")
+        tab_s = held([P, T], U8, "tab_s")
+        for q in range(4):
+            nc.sync.dma_start(
+                tab_s[32 * q : 32 * (q + 1), :].bitcast(I32),
+                tab_scales[0, 4 * q : 4 * q + 4, :].bitcast(I32).unsqueeze(0).to_broadcast([8, 4, T // 4]),
+            )
+        w1_raw = [load_rows(w1[:, 256 * h : 256 * (h + 1)], "w1_raw%d" % h) for h in range(2)]
+        tab_w = load_words(tab_words[0], "tab_w", "buf_a")
+        offs2_t = load_list(offs2, "offs2_t")
+        tab2_s = load_scales(tab2_scales, "tab2_s", nc.gpsimd, nc.sync)
+        tab2_w = [load_words(tab2_words[0], "tab2_w0", "buf_b0")]
+        w3_w = held([P, 2 * N], U8, "w3_w")
+        nc.sync.dma_start(w3_w[:].bitcast(I32), w3_words[0].bitcast(I32))
+        pages = [load_page(0)]
+        w3_s = load_scales(w3_scales, "w3_s", nc.gpsimd, nc.sync)
+        offs3_t = load_list(offs3, "offs3_t")
+        wg1_t = held([P, S], F32, "wg1_t")
+        nc.sync.dma_start(wg1_t[:, :BANK], wg1[:, :BANK])
+        tab2_w.append(load_words(tab2_words[1], "tab2_w1", "buf_b1"))
+        nc.sync.dma_start(wg1_t[:, BANK:], wg1[:, BANK:])
+        pos1_t = load_list(pos1, "pos1_t")
+        w2_raw = [load_rows(w2[512 * a : 512 * (a + 1), :], "w2_raw%d" % a) for a in range(2)]
+        gain_t = held([P, PACK], F32, "gain_t")
+        nc.sync.dma_start(gain_t[:], gain.rearrange("(p t) -> p t", t=PACK))
+        w4_raw = load_rows(w4, "w4_raw", "buf_c")
+        pages.append(load_page(1))
+        pages.append(load_page(2))
+        w5_s = load_scales(w5_scales, "w5_s", nc.gpsimd, nc.sync)
+        w5_w = [load_words(w5_words[a], "w5_w%d" % a) for a in range(2)]
+        offs4_t = load_list(offs4, "offs4_t")
+        wg2_t = held([P, PM], F32, "wg2_t")
+        nc.sync.dma_start(wg2_t[:], wg2)
+        pages.append(load_page(3))
+        ident = held([P, P], F32, "ident")
+        make_identity(nc, ident[:])
+
+        v_s = held([P, S], U8, "v_s")
+        nc.vector.tensor_copy(v_s[:], tab_s[:].indirect(offs_t[:]))
+
+        w1_g = held([P, H, PACK], BF16, "w1_g")
+        for h in range(2):
+            nc.scalar.copy(
+                w1_g[:].rearrange("p (t m) i -> p m t i", t=PACK)[:, 64 * h : 64 * (h + 1)],
+                w1_raw[h][:].rearrange("p i (m t) -> p m t i", t=PACK),
+            )
+        w1_c, w1_s = quantize(w1_g[:], "w1")
+
+        v_w = held([P, S], U32, "v_w")
+        for cols in (slice(0, 256), slice(256, S)):
+            nc.vector.tensor_copy(
+                v_w[:, cols], tab_w[:].bitcast(U32).indirect(offs_t[:, cols.start // 16 : cols.stop // 16])
+            )
+
+        v2_s = held([P, PM], U8, "v2_s")
+        nc.vector.tensor_copy(v2_s[:], tab2_s[:].indirect(offs2_t[:]))
+
+        def gather_merchants(a, tag=None):
+            gw = held([P, PM], U32, "v2_w%d" % a, tag)
+            nc.vector.tensor_copy(gw[:], tab2_w[a][:].bitcast(U32).indirect(offs2_t[:]))
+            return gw
+
+        v2_w = [gather_merchants(0)]
+
+        h1 = held([P, PACK, S], F32, "h1")
+        y1 = []
+
+        def y1_pair(tag=None):
+            pair = held([P, 2, S], F32, "y1_pair%d" % len(y1), tag)
+            y1.extend(pair[:, i, :] for i in range(2))
+
+        y1_pair()
+
+        z1_c = held([P, S], U32, "z1_c")
+        z1_s = held([P, S], U8, "z1_s")
+
+        def y1_product(n, cols):
+            bank = ps_b.tile([P, cols.stop - cols.start], F32, name="bank_b")
+            nc.tensor.matmul_mx(
+                out=bank[:],
+                lhsT=w3_w[:, 2 * P * n : 2 * P * (n + 1)].bitcast(E2M1),
+                lhsT_scale=w3_s[:, P * n : P * (n + 1)],
+                rhs=z1_c[:, cols].bitcast(E4M3),
+                rhs_scale=z1_s[:, cols],
+                start=True,
+                stop=True,
+            )
+            nc.scalar.copy(y1[n][:, cols], bank[:])
+
+        def scatter(n, offsets, values, weights):
+            nc.vector.tensor_tensor(pages[n][:].indirect(offsets), values, weights, ALU.mult)
+
+        for chunk in (slice(0, 256), slice(256, 512), slice(512, 1024)):
+            banks = []
+            z1_g = held([P, chunk.stop - chunk.start, PACK], BF16, "z1_g%d" % chunk.start)
+            for c in range(chunk.start, chunk.stop, P):
+                cols = slice(c, c + P)
+                bank = ps_a.tile([P, PACK, P], F32, name="bank_a")
+                for t in range(PACK):
+                    nc.tensor.matmul_mx(
+                        out=bank[:, t, :],
+                        lhsT=w1_c[:, P * t : P * (t + 1)].bitcast(E4M3),
+                        lhsT_scale=w1_s[:, P * t : P * (t + 1)],
+                        rhs=v_w[:, cols].bitcast(E4M3),
+                        rhs_scale=v_s[:, cols],
+                        start=True,
+                        stop=True,
+                    )
+                nc.scalar.activation(z1_g[:, c - chunk.start : c - chunk.start + P, :], bank[:].rearrange("p t j -> p j t"), ACT.Abs)
+                banks.append((cols, bank))
+            nc.vector.quantize_mx(
+                out=z1_c[:, chunk].bitcast(E4M3),
+                scales=z1_s[:, chunk],
+                in_=z1_g[:].rearrange("p c i -> p (c i)"),
+            )
+            y1_product(0, chunk)
+            scatter(0, offs3_t[:, chunk.start // 16 : chunk.stop // 16], y1[0][:, chunk], wg1_t[:, chunk])
+            for cols, bank in banks:
+                nc.scalar.copy(h1[:, :, cols], bank[:])
+
+        v2_w.append(gather_merchants(1, "z1_g0"))
+        y1_pair("buf_b0")
+        y1_pair("buf_b1")
+
+        def y1_tile(n):
+            for h in range(2):
+                y1_product(n, slice(BANK * h, BANK * (h + 1)))
+
+        y1_tile(1)
+
+        w2_q = []
+        for a in range(2):
+            w2_g = held([P, H, PACK], BF16, "w2_g%d" % a)
+            interleave(w2_g[:], w2_raw[a][:])
+            w2_q.append(quantize(w2_g[:], "w2_%d" % a))
+
+        pages.extend(load_page(4 + a, "w2_raw%d" % a) for a in range(2))
+        scatter(1, offs3_t[:], y1[1], wg1_t[:])
+        y1_tile(2)
+
+        suspect = held([P, PACK, PM], F32, "suspect")
+        for t in range(PACK):
+            nc.vector.tensor_copy(suspect[:, t, :], h1[:, t, :].indirect(pos1_t[:]))
+
+        turns = held([P, 4, H], F32, "turns", "buf_d")
+        whole = held([P, 4, H], U32, "whole", "buf_a")
+        minus = held([P, 4, H], F32, "minus")
+        for jt in range(4):
+            cols = slice(P * jt, P * (jt + 1))
+            bank = ps_a.tile([P, BANK], F32, name="bank_a")
+            for a in range(2):
+                nc.tensor.matmul_mx(
+                    out=bank[:],
+                    lhsT=v2_w[a][:, cols].bitcast(E4M3),
+                    lhsT_scale=v2_s[4 * a :, cols],
+                    rhs=w2_q[a][0][:].bitcast(E4M3),
+                    rhs_scale=w2_q[a][1][:],
+                    start=(a == 0),
+                    stop=(a == 1),
+                )
+            nc.scalar.activation(
+                turns[:, jt, :].rearrange("p (t m) -> p t m", t=PACK),
+                bank[:].rearrange("p (m t) -> p t m", t=PACK),
+                ACT.Copy,
+                scale=1.0 / (2.0 * math.pi),
+            )
+            nc.scalar.activation(whole[:, jt, :], turns[:, jt, :], ACT.Copy, bias=ROUNDER, scale=1.0)
+            nc.scalar.activation(minus[:, jt, :], whole[:, jt, :], ACT.Copy, bias=ROUNDER, scale=-1.0)
+
+        def add_turned(bank, first, second):
+            for i, src in enumerate((first, second)):
+                nc.tensor.matmul(bank, lhsT=src, rhs=ident[:], start=(i == 0), stop=(i == 1), is_transpose=True)
+
+        sine = held([P, PACK, PM], F32, "sine", "buf_e")
+        gained = held([P, PACK, PM], F32, "gained", "buf_a")
+        for t in range(PACK):
+            bank = ps_a.tile([P, BANK], F32, name="bank_a")
+            rows = slice(P * t, P * (t + 1))
+            for jt in range(4):
+                add_turned(bank[:, P * jt : P * (jt + 1)], turns[:, jt, rows], minus[:, jt, rows])
+            nc.scalar.activation(sine[:, t, :], bank[:], ACT.Sin, scale=-2.0 * math.pi)
+            nc.scalar.activation(gained[:, t, :], sine[:, t, :], ACT.Copy, scale=gain_t[:, t : t + 1])
+
+        w4_g = held([P, N, PACK], BF16, "w4_g")
+        interleave(w4_g[:], w4_raw[:])
+        w4_q = [quantize(w4_g[:, 384 * h : 384 * (h + 1), :], "w4_%d" % h) for h in range(2)]
+
+        scatter(2, offs3_t[:], y1[2], wg1_t[:])
+        y1_tile(3)
+        scatter(3, offs3_t[:], y1[3], wg1_t[:])
+
+        z2_t = held([P, 4, 2, P, 2], BF16, "z2_t", "buf_e")
+        z2_g = held([P, PM, PACK], BF16, "z2_g")
+        for jt in range(4):
+            cols = slice(P * jt, P * (jt + 1))
+            bank = ps_a.tile([P, PACK, P], F32, name="bank_a")
+            for t in range(PACK):
+                add_turned(bank[:, t, :], gained[:, t, cols], suspect[:, t, cols])
+            nc.scalar.activation(
+                z2_t[:, jt], bank[:].rearrange("j (u e) p -> j u p e", e=2), ACT.Copy, scale=-1.0
+            )
+        z2_t_words = z2_t[:].rearrange("j a u p e -> j a u (p e)").bitcast(F32)
+        z2_g_words = z2_g[:].bitcast(F32).rearrange("p (a j) u -> p a j u", j=P)
+        for h in range(2):
+            bank = ps_a.tile([P, 2, 2, P], F32, name="bank_a")
+            for a in range(2):
+                for u in range(2):
+                    nc.tensor.transpose(bank[:, a, u, :], z2_t_words[:, 2 * h + a, u, :], ident[:])
+            nc.scalar.copy(z2_g_words[:, 2 * h : 2 * h + 2], bank[:].rearrange("p a u j -> p a j u"))
+        y1_tile(4)
+        y1_tile(5)
+
+        direct = held([P, N_TILES, PM], F32, "direct", "buf_c")
+        for n in range(N_TILES):
+            cols = slice(P * n, P * (n + 1))
+            bank = ps_b.tile([P, BANK], F32, name="bank_b")
+            for a in range(2):
+                nc.tensor.matmul_mx(
+                    out=bank[:],
+                    lhsT=w5_w[a][:, cols].bitcast(E4M3),
+                    lhsT_scale=w5_s[4 * a :, cols],
+                    rhs=v2_w[a][:].bitcast(E4M3),
+                    rhs_scale=v2_s[4 * a :, :],
+                    start=(a == 0),
+                    stop=(a == 1),
+                )
+            nc.scalar.copy(direct[:, n, :], bank[:])
+
+        scatter(4, offs3_t[:], y1[4], wg1_t[:])
+        z2_c, z2_s = quantize(z2_g[:], "z2")
+        scatter(5, offs3_t[:], y1[5], wg1_t[:])
+
+        def larger(n):
+            cols = slice(P * (n % 3), P * (n % 3 + 1))
+            bank = ps_a.tile([P, BANK], F32, name="bank_a")
+            nc.tensor.matmul_mx(
+                out=bank[:],
+                lhsT=w4_q[n // 3][0][:, cols].bitcast(E4M3),
+                lhsT_scale=w4_q[n // 3][1][:, cols],
+                rhs=z2_c[:].bitcast(E4M3),
+                rhs_scale=z2_s[:],
+                start=True,
+                stop=True,
+            )
+            y2 = ring.tile([P, PM], F32, name="y2")
+            nc.vector.tensor_tensor(y2[:], bank[:], direct[:, n, :], ALU.max)
+            return y2
+
+        y2 = larger(0)
+        for n in range(N_TILES):
+            ahead = larger(n + 1) if n + 1 < N_TILES else None
+            scatter(n, offs4_t[:], y2[:], wg2_t[:])
+            nc.sync.dma_start(out[P * n : P * (n + 1), :], pages[n][:])
+            y2 = ahead

@@ -33,21 +33,42 @@ def tile_list_fraud_review_page_kernel(
     with ExitStack() as ctx:
         lists = ctx.enter_context(tc.tile_pool(name="lists", bufs=1))
         sb = ctx.enter_context(tc.tile_pool(name="sb", bufs=1))
-        ring = ctx.enter_context(tc.tile_pool(name="ring", bufs=3))
-        ps_a = ctx.enter_context(tc.psum_pool(name="ps_a", bufs=4))
-        ps_b = ctx.enter_context(tc.psum_pool(name="ps_b", bufs=4))
+        ring = ctx.enter_context(tc.tile_pool(name="ring", bufs=4))
+        psum = ctx.enter_context(tc.psum_pool(name="psum", bufs=1))
 
-        def held(shape, dtype, name, tag=None):
-            return sb.tile(shape, dtype, name=name, tag=tag or name, align_bytes=64)
+        places = {"end": 0}
+
+        def held(shape, dtype, name, over=None, skip=0):
+            if over is None:
+                size = 1 if dtype == U8 else 2 if dtype == BF16 else 4
+                for extent in shape[1:]:
+                    size = size * extent
+                places[name] = places["end"]
+                places["end"] = places["end"] + (size + 63) // 64 * 64
+            else:
+                places[name] = places[over] + skip
+            return sb.tile(shape, dtype, name=name, align_bytes=64, offset=places[name])
+
+        def take_bank(b, *shape):
+            return psum.tile([P, *shape], F32, name="bank%d" % b)
 
         def load_list(src, name):
             t = lists.tile(list(src.shape), U16, name=name)
             nc.sync.dma_start(t[:], src)
             return t
 
-        def load_words(src, name, tag=None):
-            t = held([P, src.shape[1]], I32, name, tag)
-            nc.sync.dma_start(t[:], src.rearrange("p c i -> p (c i)").bitcast(I32))
+        def load_halves(t, src):
+            half = src.shape[1] // 2
+            for c in (0, half):
+                nc.sync.dma_start(t[:, c : c + half], src[:, c : c + half])
+
+        def load_words(src, name, split=False):
+            t = held([P, src.shape[1]], I32, name)
+            words = src.rearrange("p c i -> p (c i)").bitcast(I32)
+            if split:
+                load_halves(t, words)
+            else:
+                nc.sync.dma_start(t[:], words)
             return t
 
         def load_scales(src, name, zero_engine, queue):
@@ -61,21 +82,23 @@ def tile_list_fraud_review_page_kernel(
                 )
             return t
 
-        def load_rows(rows, name, tag=None):
-            t = held([P, PACK, rows.shape[1]], F32, name, tag)
+        def load_rows(rows, name, over=None):
+            t = held([P, PACK, rows.shape[1]], F32, name, over)
             nc.sync.dma_start(t[:], rows.rearrange("(p i) c -> p i c", i=PACK))
             return t
 
-        def load_page(n, tag=None):
-            t = held([P, L], F32, "page%d" % n, tag)
+        def load_page(n, over=None):
+            t = held([P, L], F32, "page%d" % n, over)
             nc.sync.dma_start(t[:], page1[P * n : P * (n + 1), :])
             return t
 
-        def interleave(dst, src):
-            nc.scalar.copy(
-                dst.rearrange("p (c e) i -> p c i e", e=4),
-                src.rearrange("p i (c e) -> p c i e", e=4),
-            )
+        def interleave(dst, src, pieces):
+            width = dst.shape[1] // pieces
+            for c in range(0, dst.shape[1], width):
+                nc.scalar.copy(
+                    dst[:, c : c + width, :].rearrange("p (c e) i -> p c i e", e=4),
+                    src[:, :, c : c + width].rearrange("p i (c e) -> p c i e", e=4),
+                )
 
         def quantize(src, name):
             width = src.shape[1]
@@ -94,25 +117,29 @@ def tile_list_fraud_review_page_kernel(
                 tab_scales[0, 4 * q : 4 * q + 4, :].bitcast(I32).unsqueeze(0).to_broadcast([8, 4, T // 4]),
             )
         w1_raw = [load_rows(w1[:, 256 * h : 256 * (h + 1)], "w1_raw%d" % h) for h in range(2)]
-        tab_w = load_words(tab_words[0], "tab_w", "buf_a")
-        offs2_t = load_list(offs2, "offs2_t")
-        tab2_s = load_scales(tab2_scales, "tab2_s", nc.gpsimd, nc.sync)
-        tab2_w = [load_words(tab2_words[0], "tab2_w0", "buf_b0")]
+        tab_w = load_words(tab_words[0], "tab_w")
         w3_w = held([P, 2 * N], U8, "w3_w")
         nc.sync.dma_start(w3_w[:].bitcast(I32), w3_words[0].bitcast(I32))
-        pages = [load_page(0)]
         w3_s = load_scales(w3_scales, "w3_s", nc.gpsimd, nc.sync)
+        pages = [held([P, L], F32, "page0")]
+        load_halves(pages[0], page1[:P, :])
+        tab2_w = [held([P, T], I32, "tab2_w0")]
+        words0 = tab2_words[0].rearrange("p c i -> p (c i)").bitcast(I32)
+        nc.sync.dma_start(tab2_w[0][:, : T // 2], words0[:, : T // 2])
         offs3_t = load_list(offs3, "offs3_t")
         wg1_t = held([P, S], F32, "wg1_t")
-        nc.sync.dma_start(wg1_t[:, :BANK], wg1[:, :BANK])
-        tab2_w.append(load_words(tab2_words[1], "tab2_w1", "buf_b1"))
-        nc.sync.dma_start(wg1_t[:, BANK:], wg1[:, BANK:])
+        nc.sync.dma_start(wg1_t[:, :256], wg1[:, :256])
+        nc.sync.dma_start(tab2_w[0][:, T // 2 :], words0[:, T // 2 :])
+        offs2_t = load_list(offs2, "offs2_t")
+        tab2_s = load_scales(tab2_scales, "tab2_s", nc.gpsimd, nc.sync)
+        nc.sync.dma_start(wg1_t[:, 256:], wg1[:, 256:])
+        tab2_w.append(load_words(tab2_words[1], "tab2_w1", True))
         pos1_t = load_list(pos1, "pos1_t")
         w2_raw = [load_rows(w2[512 * a : 512 * (a + 1), :], "w2_raw%d" % a) for a in range(2)]
+        pages.append(load_page(1))
         gain_t = held([P, PACK], F32, "gain_t")
         nc.sync.dma_start(gain_t[:], gain.rearrange("(p t) -> p t", t=PACK))
-        w4_raw = load_rows(w4, "w4_raw", "buf_c")
-        pages.append(load_page(1))
+        w4_raw = load_rows(w4, "w4_raw")
         pages.append(load_page(2))
         w5_s = load_scales(w5_scales, "w5_s", nc.gpsimd, nc.sync)
         w5_w = [load_words(w5_words[a], "w5_w%d" % a) for a in range(2)]
@@ -134,56 +161,62 @@ def tile_list_fraud_review_page_kernel(
             )
         w1_c, w1_s = quantize(w1_g[:], "w1")
 
-        v_w = held([P, S], U32, "v_w")
+        v_w = held([P, S], U32, "v_w", "w1_g")
         for cols in (slice(0, 256), slice(256, S)):
             nc.vector.tensor_copy(
                 v_w[:, cols], tab_w[:].bitcast(U32).indirect(offs_t[:, cols.start // 16 : cols.stop // 16])
             )
 
-        v2_s = held([P, PM], U8, "v2_s")
-        nc.vector.tensor_copy(v2_s[:], tab2_s[:].indirect(offs2_t[:]))
-
-        def gather_merchants(a, tag=None):
-            gw = held([P, PM], U32, "v2_w%d" % a, tag)
+        def gather_merchants(a, over, skip=0):
+            gw = held([P, PM], U32, "v2_w%d" % a, over, skip)
             nc.vector.tensor_copy(gw[:], tab2_w[a][:].bitcast(U32).indirect(offs2_t[:]))
             return gw
 
-        v2_w = [gather_merchants(0)]
+        v2_w = []
 
         h1 = held([P, PACK, S], F32, "h1")
-        y1 = []
+        places["w2_g_place"] = places["end"]
+        places["end"] = places["end"] + 10240
+        y1 = [None]
 
-        def y1_pair(tag=None):
-            pair = held([P, 2, S], F32, "y1_pair%d" % len(y1), tag)
-            y1.extend(pair[:, i, :] for i in range(2))
-
-        y1_pair()
-
-        z1_c = held([P, S], U32, "z1_c")
+        chunks = (slice(0, 256), slice(256, 512), slice(512, 1024))
+        places["end"] = places["end"] + 1536
+        first = {c.start: held([P, c.stop - c.start], F32, "y1_0_%d" % c.start) for c in chunks}
+        z1_c = [held([P, BANK], U32, "z1_c0")]
         z1_s = held([P, S], U8, "z1_s")
 
-        def y1_product(n, cols):
-            bank = ps_b.tile([P, cols.stop - cols.start], F32, name="bank_b")
+        def z1_codes(cols):
+            h = cols.start // BANK
+            return z1_c[h][:, cols.start - BANK * h : cols.stop - BANK * h].bitcast(E4M3)
+
+        def y1_product(n, cols, b, stage):
+            bank = take_bank(b, cols.stop - cols.start)
             nc.tensor.matmul_mx(
                 out=bank[:],
                 lhsT=w3_w[:, 2 * P * n : 2 * P * (n + 1)].bitcast(E2M1),
                 lhsT_scale=w3_s[:, P * n : P * (n + 1)],
-                rhs=z1_c[:, cols].bitcast(E4M3),
+                rhs=z1_codes(cols),
                 rhs_scale=z1_s[:, cols],
                 start=True,
                 stop=True,
             )
-            nc.scalar.copy(y1[n][:, cols], bank[:])
+            nc.scalar.copy(stage, bank[:])
 
         def scatter(n, offsets, values, weights):
             nc.vector.tensor_tensor(pages[n][:].indirect(offsets), values, weights, ALU.mult)
 
-        for chunk in (slice(0, 256), slice(256, 512), slice(512, 1024)):
-            banks = []
-            z1_g = held([P, chunk.stop - chunk.start, PACK], BF16, "z1_g%d" % chunk.start)
+        banks = []
+
+        def keep_h1(b):
+            nc.scalar.copy(h1[:, :, P * b : P * (b + 1)], banks[b][:])
+
+        for chunk in chunks:
+            z1_g = held([P, chunk.stop - chunk.start, PACK], BF16, "z1_g%d" % chunk.start, *(("w2_g_place", 3072) if chunk.stop == S else ()))
             for c in range(chunk.start, chunk.stop, P):
                 cols = slice(c, c + P)
-                bank = ps_a.tile([P, PACK, P], F32, name="bank_a")
+                if len(banks) == 2:
+                    keep_h1(0)
+                bank = take_bank(len(banks) % 7, PACK, P)
                 for t in range(PACK):
                     nc.tensor.matmul_mx(
                         out=bank[:, t, :],
@@ -195,47 +228,56 @@ def tile_list_fraud_review_page_kernel(
                         stop=True,
                     )
                 nc.scalar.activation(z1_g[:, c - chunk.start : c - chunk.start + P, :], bank[:].rearrange("p t j -> p j t"), ACT.Abs)
-                banks.append((cols, bank))
+                banks.append(bank)
+            if chunk.start == BANK:
+                z1_c.append(held([P, BANK], U32, "z1_c1", "y1_0_0", -1536))
             nc.vector.quantize_mx(
-                out=z1_c[:, chunk].bitcast(E4M3),
+                out=z1_codes(chunk),
                 scales=z1_s[:, chunk],
                 in_=z1_g[:].rearrange("p c i -> p (c i)"),
             )
-            y1_product(0, chunk)
-            scatter(0, offs3_t[:, chunk.start // 16 : chunk.stop // 16], y1[0][:, chunk], wg1_t[:, chunk])
-            for cols, bank in banks:
-                nc.scalar.copy(h1[:, :, cols], bank[:])
+            y1_product(0, chunk, 7, first[chunk.start][:])
+            scatter(0, offs3_t[:, chunk.start // 16 : chunk.stop // 16], first[chunk.start][:], wg1_t[:, chunk])
+            if chunk.start == 256:
+                v2_s = held([P, PM], U8, "v2_s", "y1_0_0", 512)
+                nc.vector.tensor_copy(v2_s[:], tab2_s[:].indirect(offs2_t[:]))
+                v2_w.append(gather_merchants(0, "z1_g256"))
 
-        v2_w.append(gather_merchants(1, "z1_g0"))
-        y1_pair("buf_b0")
-        y1_pair("buf_b1")
+        v2_w.append(gather_merchants(1, "w2_g_place", 4096))
 
-        def y1_tile(n):
+        def y1_tile(n, pair, over, skip=0):
+            y1.append(held([P, S], F32, "y1_%d" % n, over, skip))
             for h in range(2):
-                y1_product(n, slice(BANK * h, BANK * (h + 1)))
+                y1_product(n, slice(BANK * h, BANK * (h + 1)), pair[h], y1[n][:, BANK * h : BANK * (h + 1)])
 
-        y1_tile(1)
+        keep_h1(1)
 
+        w2_g = [held([P, H, PACK], BF16, "w2_g%d" % a, "w2_g_place", 6144 * a) for a in range(2)]
         w2_q = []
         for a in range(2):
-            w2_g = held([P, H, PACK], BF16, "w2_g%d" % a)
-            interleave(w2_g[:], w2_raw[a][:])
-            w2_q.append(quantize(w2_g[:], "w2_%d" % a))
+            interleave(w2_g[a][:], w2_raw[a][:], 2)
+            w2_q.append(quantize(w2_g[a][:], "w2_%d" % a))
 
-        pages.extend(load_page(4 + a, "w2_raw%d" % a) for a in range(2))
-        scatter(1, offs3_t[:], y1[1], wg1_t[:])
-        y1_tile(2)
+        y1_tile(1, (7, 1), "w2_raw1")
+        scatter(1, offs3_t[:], y1[1][:], wg1_t[:])
+        for b in (4, 5, 6, 7, 2, 3):
+            keep_h1(b)
+        pages.append(load_page(4))
+        pages.append(load_page(5, "tab2_w1"))
+        suspect = []
+        for a in range(2):
+            pair = held([P, 2, PM], F32, "suspect%d" % a, "w2_g%d" % a)
+            for e in range(2):
+                nc.vector.tensor_copy(pair[:, e, :], h1[:, 2 * a + e, :].indirect(pos1_t[:]))
+                suspect.append(pair[:, e, :])
+        y1_tile(2, (7, 1), "w2_raw1", 4096)
 
-        suspect = held([P, PACK, PM], F32, "suspect")
-        for t in range(PACK):
-            nc.vector.tensor_copy(suspect[:, t, :], h1[:, t, :].indirect(pos1_t[:]))
-
-        turns = held([P, 4, H], F32, "turns", "buf_d")
-        whole = held([P, 4, H], U32, "whole", "buf_a")
+        turns = held([P, 4, H], F32, "turns")
+        whole = held([P, 4, H], U32, "whole", "w1_raw0")
         minus = held([P, 4, H], F32, "minus")
         for jt in range(4):
             cols = slice(P * jt, P * (jt + 1))
-            bank = ps_a.tile([P, BANK], F32, name="bank_a")
+            bank = take_bank((4, 5, 6, 0)[jt], BANK)
             for a in range(2):
                 nc.tensor.matmul_mx(
                     out=bank[:],
@@ -255,14 +297,23 @@ def tile_list_fraud_review_page_kernel(
             nc.scalar.activation(whole[:, jt, :], turns[:, jt, :], ACT.Copy, bias=ROUNDER, scale=1.0)
             nc.scalar.activation(minus[:, jt, :], whole[:, jt, :], ACT.Copy, bias=ROUNDER, scale=-1.0)
 
+        scatter(2, offs3_t[:], y1[2][:], wg1_t[:])
+        y1_tile(3, (2, 3), "w2_raw0")
+        scatter(3, offs3_t[:], y1[3][:], wg1_t[:])
+        halves = [slice(0, BANK), slice(BANK, S)]
+        y1_4 = [held([P, BANK], F32, "y1_4a", "w2_raw0", 4096)]
+        y1_product(4, halves[0], 2, y1_4[0][:])
+        scatter(4, offs3_t[:, :32], y1_4[0][:], wg1_t[:, halves[0]])
+        y1.append(None)
+
         def add_turned(bank, first, second):
             for i, src in enumerate((first, second)):
                 nc.tensor.matmul(bank, lhsT=src, rhs=ident[:], start=(i == 0), stop=(i == 1), is_transpose=True)
 
-        sine = held([P, PACK, PM], F32, "sine", "buf_e")
-        gained = held([P, PACK, PM], F32, "gained", "buf_a")
+        sine = held([P, PACK, PM], F32, "sine")
+        gained = held([P, PACK, PM], F32, "gained", "whole")
         for t in range(PACK):
-            bank = ps_a.tile([P, BANK], F32, name="bank_a")
+            bank = take_bank((7, 1, 2, 3)[t], BANK)
             rows = slice(P * t, P * (t + 1))
             for jt in range(4):
                 add_turned(bank[:, P * jt : P * (jt + 1)], turns[:, jt, rows], minus[:, jt, rows])
@@ -270,38 +321,37 @@ def tile_list_fraud_review_page_kernel(
             nc.scalar.activation(gained[:, t, :], sine[:, t, :], ACT.Copy, scale=gain_t[:, t : t + 1])
 
         w4_g = held([P, N, PACK], BF16, "w4_g")
-        interleave(w4_g[:], w4_raw[:])
+        interleave(w4_g[:], w4_raw[:], 4)
         w4_q = [quantize(w4_g[:, 384 * h : 384 * (h + 1), :], "w4_%d" % h) for h in range(2)]
 
-        scatter(2, offs3_t[:], y1[2], wg1_t[:])
-        y1_tile(3)
-        scatter(3, offs3_t[:], y1[3], wg1_t[:])
 
-        z2_t = held([P, 4, 2, P, 2], BF16, "z2_t", "buf_e")
+        z2_t = held([P, 4, 2, P, 2], BF16, "z2_t", "sine", 2048)
         z2_g = held([P, PM, PACK], BF16, "z2_g")
         for jt in range(4):
             cols = slice(P * jt, P * (jt + 1))
-            bank = ps_a.tile([P, PACK, P], F32, name="bank_a")
+            bank = take_bank((4, 5, 6, 0)[jt], PACK, P)
             for t in range(PACK):
-                add_turned(bank[:, t, :], gained[:, t, cols], suspect[:, t, cols])
+                add_turned(bank[:, t, :], gained[:, t, cols], suspect[t][:, cols])
             nc.scalar.activation(
                 z2_t[:, jt], bank[:].rearrange("j (u e) p -> j u p e", e=2), ACT.Copy, scale=-1.0
             )
         z2_t_words = z2_t[:].rearrange("j a u p e -> j a u (p e)").bitcast(F32)
         z2_g_words = z2_g[:].bitcast(F32).rearrange("p (a j) u -> p a j u", j=P)
         for h in range(2):
-            bank = ps_a.tile([P, 2, 2, P], F32, name="bank_a")
+            bank = take_bank((7, 1)[h], 2, 2, P)
             for a in range(2):
                 for u in range(2):
                     nc.tensor.transpose(bank[:, a, u, :], z2_t_words[:, 2 * h + a, u, :], ident[:])
             nc.scalar.copy(z2_g_words[:, 2 * h : 2 * h + 2], bank[:].rearrange("p a u j -> p a j u"))
-        y1_tile(4)
-        y1_tile(5)
+        y1_4.append(held([P, BANK], F32, "y1_4b", "sine", 1024))
+        y1_product(4, halves[1], 6, y1_4[1][:])
+        y1_tile(5, (4, 5), "sine", 3072)
 
-        direct = held([P, N_TILES, PM], F32, "direct", "buf_c")
-        for n in range(N_TILES):
+        minus_b, b_turned = [], []
+
+        def direct(n):
             cols = slice(P * n, P * (n + 1))
-            bank = ps_b.tile([P, BANK], F32, name="bank_b")
+            bank = take_bank(2 + n % 2, BANK)
             for a in range(2):
                 nc.tensor.matmul_mx(
                     out=bank[:],
@@ -312,15 +362,25 @@ def tile_list_fraud_review_page_kernel(
                     start=(a == 0),
                     stop=(a == 1),
                 )
-            nc.scalar.copy(direct[:, n, :], bank[:])
+            over = ("tab2_w0", 2048 * n) if n < 4 else ("tab_w", 2048 * (n - 2))
+            minus_b.append(held([P, PM], F32, "minus_b%d" % n, *over))
+            nc.scalar.activation(minus_b[n][:], bank[:], ACT.Copy, scale=-1.0)
+            bank = take_bank(4 + n % 2, 4, P)
+            for jt in range(4):
+                nc.tensor.transpose(bank[:, jt, :], minus_b[n][:, P * jt : P * (jt + 1)], ident[:])
+            over = ("turns", 2048 * n) if n < 4 else ("minus", 2048 * (n - 4))
+            b_turned.append(held([P, 4, P], F32, "b_turned%d" % n, *over))
+            nc.scalar.activation(b_turned[n][:], bank[:], ACT.Copy, scale=-1.0)
 
-        scatter(4, offs3_t[:], y1[4], wg1_t[:])
+        for n in range(3):
+            direct(n)
         z2_c, z2_s = quantize(z2_g[:], "z2")
-        scatter(5, offs3_t[:], y1[5], wg1_t[:])
+        scatter(4, offs3_t[:, 32:], y1_4[1][:], wg1_t[:, halves[1]])
+        scatter(5, offs3_t[:], y1[5][:], wg1_t[:])
 
         def larger(n):
             cols = slice(P * (n % 3), P * (n % 3 + 1))
-            bank = ps_a.tile([P, BANK], F32, name="bank_a")
+            bank = take_bank((4, 2, 5, 3)[n % 4], BANK)
             nc.tensor.matmul_mx(
                 out=bank[:],
                 lhsT=w4_q[n // 3][0][:, cols].bitcast(E4M3),
@@ -330,13 +390,24 @@ def tile_list_fraud_review_page_kernel(
                 start=True,
                 stop=True,
             )
+            a_sb = held([P, PM], F32, "a_sb%d" % n, "gained", 2048 * (n % 2))
+            nc.scalar.copy(a_sb[:], bank[:])
+            bank = take_bank((7, 1)[n % 2], 4, P)
+            for jt in range(4):
+                cols = slice(P * jt, P * (jt + 1))
+                add_turned(bank[:, jt, :], a_sb[:, cols], minus_b[n][:, cols])
+            excess = held([P, 4, P], F32, "excess%d" % n, "gained", 4096 + 2048 * (n % 2))
+            nc.scalar.activation(excess[:], bank[:], ACT.Relu)
+            bank = take_bank((6, 0)[n % 2], 4, P)
+            for jt in range(4):
+                add_turned(bank[:, jt, :], excess[:, jt, :], b_turned[n][:, jt, :])
             y2 = ring.tile([P, PM], F32, name="y2")
-            nc.vector.tensor_tensor(y2[:], bank[:], direct[:, n, :], ALU.max)
+            nc.scalar.copy(y2[:], bank[:].rearrange("p a j -> p (a j)"))
             return y2
 
-        y2 = larger(0)
         for n in range(N_TILES):
-            ahead = larger(n + 1) if n + 1 < N_TILES else None
+            y2 = larger(n)
             scatter(n, offs4_t[:], y2[:], wg2_t[:])
             nc.sync.dma_start(out[P * n : P * (n + 1), :], pages[n][:])
-            y2 = ahead
+            if n + 3 < N_TILES:
+                direct(n + 3)

@@ -116,21 +116,18 @@ def tile_list_fraud_review_page_kernel(
                 tab_s[32 * q : 32 * (q + 1), :].bitcast(I32),
                 tab_scales[0, 4 * q : 4 * q + 4, :].bitcast(I32).unsqueeze(0).to_broadcast([8, 4, T // 4]),
             )
-        w1_raw = [load_rows(w1[:, 256 * h : 256 * (h + 1)], "w1_raw%d" % h) for h in range(2)]
+        offs2_t = load_list(offs2, "offs2_t")
+        w1_raw = load_rows(w1, "w1_raw0")
         tab_w = load_words(tab_words[0], "tab_w")
         w3_w = held([P, 2 * N], U8, "w3_w")
         nc.sync.dma_start(w3_w[:].bitcast(I32), w3_words[0].bitcast(I32))
         w3_s = load_scales(w3_scales, "w3_s", nc.gpsimd, nc.sync)
+        tab2_w = [load_words(tab2_words[0], "tab2_w0", True)]
         pages = [held([P, L], F32, "page0")]
         load_halves(pages[0], page1[:P, :])
-        tab2_w = [held([P, T], I32, "tab2_w0")]
-        words0 = tab2_words[0].rearrange("p c i -> p (c i)").bitcast(I32)
-        nc.sync.dma_start(tab2_w[0][:, : T // 2], words0[:, : T // 2])
         offs3_t = load_list(offs3, "offs3_t")
         wg1_t = held([P, S], F32, "wg1_t")
         nc.sync.dma_start(wg1_t[:, :256], wg1[:, :256])
-        nc.sync.dma_start(tab2_w[0][:, T // 2 :], words0[:, T // 2 :])
-        offs2_t = load_list(offs2, "offs2_t")
         tab2_s = load_scales(tab2_scales, "tab2_s", nc.gpsimd, nc.sync)
         nc.sync.dma_start(wg1_t[:, 256:], wg1[:, 256:])
         tab2_w.append(load_words(tab2_words[1], "tab2_w1", True))
@@ -154,10 +151,10 @@ def tile_list_fraud_review_page_kernel(
         nc.vector.tensor_copy(v_s[:], tab_s[:].indirect(offs_t[:]))
 
         w1_g = held([P, H, PACK], BF16, "w1_g")
-        for h in range(2):
-            nc.scalar.copy(
+        for h, copy in enumerate((nc.scalar.copy, nc.vector.tensor_copy)):
+            copy(
                 w1_g[:].rearrange("p (t m) i -> p m t i", t=PACK)[:, 64 * h : 64 * (h + 1)],
-                w1_raw[h][:].rearrange("p i (m t) -> p m t i", t=PACK),
+                w1_raw[:].rearrange("p i (m t) -> p m t i", t=PACK)[:, 64 * h : 64 * (h + 1)],
             )
         w1_c, w1_s = quantize(w1_g[:], "w1")
 
@@ -172,7 +169,7 @@ def tile_list_fraud_review_page_kernel(
             nc.vector.tensor_copy(gw[:], tab2_w[a][:].bitcast(U32).indirect(offs2_t[:]))
             return gw
 
-        v2_w = []
+        v2_w = [gather_merchants(0, "tab_w")]
 
         h1 = held([P, PACK, S], F32, "h1")
         places["w2_g_place"] = places["end"]
@@ -180,8 +177,7 @@ def tile_list_fraud_review_page_kernel(
         y1 = [None]
 
         chunks = (slice(0, 256), slice(256, 512), slice(512, 1024))
-        places["end"] = places["end"] + 1536
-        first = {c.start: held([P, c.stop - c.start], F32, "y1_0_%d" % c.start) for c in chunks}
+        first = {}
         z1_c = [held([P, BANK], U32, "z1_c0")]
         z1_s = held([P, S], U8, "z1_s")
 
@@ -210,7 +206,14 @@ def tile_list_fraud_review_page_kernel(
         def keep_h1(b):
             nc.scalar.copy(h1[:, :, P * b : P * (b + 1)], banks[b][:])
 
-        for chunk in chunks:
+        def stage_first(c, over=None):
+            first[c.start] = held([P, c.stop - c.start], F32, "y1_0_%d" % c.start, over)
+            y1_product(0, c, 7, first[c.start][:])
+
+        def scatter_first(c):
+            scatter(0, offs3_t[:, c.start // 16 : c.stop // 16], first[c.start][:], wg1_t[:, c])
+
+        for k, chunk in enumerate(chunks):
             z1_g = held([P, chunk.stop - chunk.start, PACK], BF16, "z1_g%d" % chunk.start, *(("w2_g_place", 3072) if chunk.stop == S else ()))
             for c in range(chunk.start, chunk.stop, P):
                 cols = slice(c, c + P)
@@ -230,27 +233,30 @@ def tile_list_fraud_review_page_kernel(
                 nc.scalar.activation(z1_g[:, c - chunk.start : c - chunk.start + P, :], bank[:].rearrange("p t j -> p j t"), ACT.Abs)
                 banks.append(bank)
             if chunk.start == BANK:
-                z1_c.append(held([P, BANK], U32, "z1_c1", "y1_0_0", -1536))
+                z1_c.append(held([P, BANK], U32, "z1_c1", "z1_g256", -1536))
             nc.vector.quantize_mx(
                 out=z1_codes(chunk),
                 scales=z1_s[:, chunk],
                 in_=z1_g[:].rearrange("p c i -> p (c i)"),
             )
-            y1_product(0, chunk, 7, first[chunk.start][:])
-            scatter(0, offs3_t[:, chunk.start // 16 : chunk.stop // 16], first[chunk.start][:], wg1_t[:, chunk])
-            if chunk.start == 256:
-                v2_s = held([P, PM], U8, "v2_s", "y1_0_0", 512)
+            if k == 1:
+                stage_first(chunks[0], "z1_g256")
+                v2_s = held([P, PM], U8, "v2_s", "z1_g256", 1536)
                 nc.vector.tensor_copy(v2_s[:], tab2_s[:].indirect(offs2_t[:]))
-                v2_w.append(gather_merchants(0, "z1_g256"))
+            if k > 0:
+                scatter_first(chunks[k - 1])
+                stage_first(chunk)
 
         v2_w.append(gather_merchants(1, "w2_g_place", 4096))
+        scatter_first(chunks[-1])
 
         def y1_tile(n, pair, over, skip=0):
             y1.append(held([P, S], F32, "y1_%d" % n, over, skip))
             for h in range(2):
                 y1_product(n, slice(BANK * h, BANK * (h + 1)), pair[h], y1[n][:, BANK * h : BANK * (h + 1)])
 
-        keep_h1(1)
+        for b in range(1, len(banks)):
+            keep_h1(b)
 
         w2_g = [held([P, H, PACK], BF16, "w2_g%d" % a, "w2_g_place", 6144 * a) for a in range(2)]
         w2_q = []
@@ -260,8 +266,6 @@ def tile_list_fraud_review_page_kernel(
 
         y1_tile(1, (7, 1), "w2_raw1")
         scatter(1, offs3_t[:], y1[1][:], wg1_t[:])
-        for b in (4, 5, 6, 7, 2, 3):
-            keep_h1(b)
         pages.append(load_page(4))
         pages.append(load_page(5, "tab2_w1"))
         suspect = []
@@ -372,7 +376,7 @@ def tile_list_fraud_review_page_kernel(
             b_turned.append(held([P, 4, P], F32, "b_turned%d" % n, *over))
             nc.scalar.activation(b_turned[n][:], bank[:], ACT.Copy, scale=-1.0)
 
-        for n in range(3):
+        for n in range(2):
             direct(n)
         z2_c, z2_s = quantize(z2_g[:], "z2")
         scatter(4, offs3_t[:, 32:], y1_4[1][:], wg1_t[:, halves[1]])
@@ -380,7 +384,7 @@ def tile_list_fraud_review_page_kernel(
 
         def larger(n):
             cols = slice(P * (n % 3), P * (n % 3 + 1))
-            bank = take_bank((4, 2, 5, 3)[n % 4], BANK)
+            bank = take_bank((6, 0)[n % 2], BANK)
             nc.tensor.matmul_mx(
                 out=bank[:],
                 lhsT=w4_q[n // 3][0][:, cols].bitcast(E4M3),
@@ -398,7 +402,7 @@ def tile_list_fraud_review_page_kernel(
                 add_turned(bank[:, jt, :], a_sb[:, cols], minus_b[n][:, cols])
             excess = held([P, 4, P], F32, "excess%d" % n, "gained", 4096 + 2048 * (n % 2))
             nc.scalar.activation(excess[:], bank[:], ACT.Relu)
-            bank = take_bank((6, 0)[n % 2], 4, P)
+            bank = take_bank((7, 1)[n % 2], 4, P)
             for jt in range(4):
                 add_turned(bank[:, jt, :], excess[:, jt, :], b_turned[n][:, jt, :])
             y2 = ring.tile([P, PM], F32, name="y2")
@@ -409,5 +413,5 @@ def tile_list_fraud_review_page_kernel(
             y2 = larger(n)
             scatter(n, offs4_t[:], y2[:], wg2_t[:])
             nc.sync.dma_start(out[P * n : P * (n + 1), :], pages[n][:])
-            if n + 3 < N_TILES:
-                direct(n + 3)
+            if n + 2 < N_TILES:
+                direct(n + 2)

@@ -151,10 +151,10 @@ def tile_list_fraud_review_page_kernel(
         nc.vector.tensor_copy(v_s[:], tab_s[:].indirect(offs_t[:]))
 
         w1_g = held([P, H, PACK], BF16, "w1_g")
-        for h, copy in enumerate((nc.scalar.copy, nc.vector.tensor_copy)):
+        for copy, part in ((nc.scalar.copy, slice(0, 40)), (nc.vector.tensor_copy, slice(40, P))):
             copy(
-                w1_g[:].rearrange("p (t m) i -> p m t i", t=PACK)[:, 64 * h : 64 * (h + 1)],
-                w1_raw[:].rearrange("p i (m t) -> p m t i", t=PACK)[:, 64 * h : 64 * (h + 1)],
+                w1_g[:].rearrange("p (t m) i -> p m t i", t=PACK)[:, part],
+                w1_raw[:].rearrange("p i (m t) -> p m t i", t=PACK)[:, part],
             )
         w1_c, w1_s = quantize(w1_g[:], "w1")
 
@@ -269,11 +269,9 @@ def tile_list_fraud_review_page_kernel(
         pages.append(load_page(4))
         pages.append(load_page(5, "tab2_w1"))
         suspect = []
-        for a in range(2):
-            pair = held([P, 2, PM], F32, "suspect%d" % a, "w2_g%d" % a)
-            for e in range(2):
-                nc.vector.tensor_copy(pair[:, e, :], h1[:, 2 * a + e, :].indirect(pos1_t[:]))
-                suspect.append(pair[:, e, :])
+        for t, over in enumerate((None, None, "w2_g0", "w2_g1")):
+            suspect.append(held([P, PM], F32, "suspect%d" % t, over))
+            nc.vector.tensor_copy(suspect[t][:], h1[:, t, :].indirect(pos1_t[:]))
         y1_tile(2, (7, 1), "w2_raw1", 4096)
 
         turns = held([P, 4, H], F32, "turns")

import math
from contextlib import ExitStack

import concourse.mybir as mybir
from concourse.masks import make_identity

K, M, H, N, T, S, PM, L = 512, 1024, 512, 768, 2048, 1024, 512, 2048
FLOPS = 2 * (K * H * S + M * H * PM + H * N * S + H * N * PM + M * N * PM)

F32 = mybir.dt.float32
BF16 = mybir.dt.bfloat16
I32 = mybir.dt.int32
U32 = mybir.dt.uint32
U16 = mybir.dt.uint16
U8 = mybir.dt.uint8
E4M3 = mybir.dt.float8_e4m3fn_x4
E2M1 = mybir.dt.float4_e2m1fn_x4
ACT = mybir.ActivationFunctionType
ALU = mybir.AluOpType

P = 128
PACK = 4
BANK = 512
N_TILES = N // P
ROUNDER = 1.5 * 2.0**23


def tile_list_fraud_review_page_kernel(
    tc, tab_words, tab_scales, tab2_words, tab2_scales, offs, offs2, pos1, offs3, offs4,
    w1, w2, gain, w3_words, w3_scales, w4, w5_words, w5_scales, page1, wg1, wg2, out,
):
    nc = tc.nc
    with ExitStack() as ctx:
        lists = ctx.enter_context(tc.tile_pool(name="lists", bufs=1))
        sb = ctx.enter_context(tc.tile_pool(name="sb", bufs=1))
        ring = ctx.enter_context(tc.tile_pool(name="ring", bufs=4))
        psum = ctx.enter_context(tc.psum_pool(name="psum", bufs=1))

        places = {"end": 0}

        def held(shape, dtype, name, over=None, skip=0):
            if over is None:
                size = 1 if dtype == U8 else 2 if dtype == BF16 else 4
                for extent in shape[1:]:
                    size = size * extent
                places[name] = places["end"]
                places["end"] = places["end"] + (size + 63) // 64 * 64
            else:
                places[name] = places[over] + skip
            return sb.tile(shape, dtype, name=name, align_bytes=64, offset=places[name])

        def take_bank(b, *shape):
            return psum.tile([P, *shape], F32, name="bank%d" % b)

        def load_list(src, name):
            t = lists.tile(list(src.shape), U16, name=name)
            nc.sync.dma_start(t[:], src)
            return t

        def load_halves(t, src):
            half = src.shape[1] // 2
            for c in (0, half):
                nc.sync.dma_start(t[:, c : c + half], src[:, c : c + half])

        def load_words(src, name, split=False):
            t = held([P, src.shape[1]], I32, name)
            words = src.rearrange("p c i -> p (c i)").bitcast(I32)
            if split:
                load_halves(t, words)
            else:
                nc.sync.dma_start(t[:], words)
            return t

        def load_scales(src, name, zero_engine, queue):
            passes, width = src.shape[0], src.shape[2]
            t = held([P, width], U8, name)
            zero_engine.memset(t[:].bitcast(I32), 0)
            for q in range(4):
                queue.dma_start(
                    t[32 * q : 32 * q + 4 * passes, :].bitcast(I32),
                    src[:, 4 * q : 4 * q + 4, :].bitcast(I32),
                )
            return t

        def load_rows(rows, name, over=None):
            t = held([P, PACK, rows.shape[1]], F32, name, over)
            nc.sync.dma_start(t[:], rows.rearrange("(p i) c -> p i c", i=PACK))
            return t

        def load_page(n, over=None):
            t = held([P, L], F32, "page%d" % n, over)
            nc.sync.dma_start(t[:], page1[P * n : P * (n + 1), :])
            return t

        def interleave(dst, src, pieces):
            width = dst.shape[1] // pieces
            for c in range(0, dst.shape[1], width):
                nc.scalar.copy(
                    dst[:, c : c + width, :].rearrange("p (c e) i -> p c i e", e=4),
                    src[:, :, c : c + width].rearrange("p i (c e) -> p c i e", e=4),
                )

        def quantize(src, name):
            width = src.shape[1]
            codes = held([P, width], U32, name + "_codes")
            scales = held([P, width], U8, name + "_scales")
            nc.vector.quantize_mx(
                out=codes[:].bitcast(E4M3), scales=scales[:], in_=src.rearrange("p c i -> p (c i)")
            )
            return codes, scales

        offs_t = load_list(offs, "offs_t")
        tab_s = held([P, T], U8, "tab_s")
        for q in range(4):
            nc.sync.dma_start(
                tab_s[32 * q : 32 * (q + 1), :].bitcast(I32),
                tab_scales[0, 4 * q : 4 * q + 4, :].bitcast(I32).unsqueeze(0).to_broadcast([8, 4, T // 4]),
            )
        offs2_t = load_list(offs2, "offs2_t")
        w1_raw = load_rows(w1, "w1_raw0")
        tab_w = load_words(tab_words[0], "tab_w")
        w3_w = held([P, 2 * N], U8, "w3_w")
        nc.sync.dma_start(w3_w[:].bitcast(I32), w3_words[0].bitcast(I32))
        w3_s = load_scales(w3_scales, "w3_s", nc.gpsimd, nc.sync)
        tab2_w = [load_words(tab2_words[0], "tab2_w0", True)]
        pages = [held([P, L], F32, "page0")]
        load_halves(pages[0], page1[:P, :])
        offs3_t = load_list(offs3, "offs3_t")
        wg1_t = held([P, S], F32, "wg1_t")
        nc.sync.dma_start(wg1_t[:, :256], wg1[:, :256])
        tab2_s = load_scales(tab2_scales, "tab2_s", nc.gpsimd, nc.sync)
        nc.sync.dma_start(wg1_t[:, 256:], wg1[:, 256:])
        tab2_w.append(load_words(tab2_words[1], "tab2_w1", True))
        pos1_t = load_list(pos1, "pos1_t")
        w2_raw = [load_rows(w2[512 * a : 512 * (a + 1), :], "w2_raw%d" % a) for a in range(2)]
        pages.append(load_page(1))
        gain_t = held([P, PACK], F32, "gain_t")
        nc.sync.dma_start(gain_t[:], gain.rearrange("(p t) -> p t", t=PACK))
        w4_raw = load_rows(w4, "w4_raw")
        pages.append(load_page(2))
        w5_s = load_scales(w5_scales, "w5_s", nc.gpsimd, nc.sync)
        w5_w = [load_words(w5_words[a], "w5_w%d" % a) for a in range(2)]
        offs4_t = load_list(offs4, "offs4_t")
        wg2_t = held([P, PM], F32, "wg2_t")
        nc.sync.dma_start(wg2_t[:], wg2)
        pages.append(load_page(3))
        ident = held([P, P], F32, "ident")
        make_identity(nc, ident[:])

        v_s = held([P, S], U8, "v_s")
        nc.vector.tensor_copy(v_s[:], tab_s[:].indirect(offs_t[:]))

        w1_g = held([P, H, PACK], BF16, "w1_g")
        for copy, part in ((nc.scalar.copy, slice(0, 40)), (nc.vector.tensor_copy, slice(40, P))):
            copy(
                w1_g[:].rearrange("p (t m) i -> p m t i", t=PACK)[:, part],
                w1_raw[:].rearrange("p i (m t) -> p m t i", t=PACK)[:, part],
            )
        w1_c, w1_s = quantize(w1_g[:], "w1")

        v_w = held([P, S], U32, "v_w", "w1_g")
        for cols in (slice(0, 256), slice(256, S)):
            nc.vector.tensor_copy(
                v_w[:, cols], tab_w[:].bitcast(U32).indirect(offs_t[:, cols.start // 16 : cols.stop // 16])
            )

        def gather_merchants(a, over, skip=0):
            gw = held([P, PM], U32, "v2_w%d" % a, over, skip)
            nc.vector.tensor_copy(gw[:], tab2_w[a][:].bitcast(U32).indirect(offs2_t[:]))
            return gw

        v2_w = [gather_merchants(0, "tab_w")]

        h1 = held([P, PACK, S], F32, "h1")
        places["w2_g_place"] = places["end"]
        places["end"] = places["end"] + 10240
        y1 = [None]

        chunks = (slice(0, 256), slice(256, 512), slice(512, 1024))
        first = {}
        z1_c = [held([P, BANK], U32, "z1_c0")]
        z1_s = held([P, S], U8, "z1_s")

        def z1_codes(cols):
            h = cols.start // BANK
            return z1_c[h][:, cols.start - BANK * h : cols.stop - BANK * h].bitcast(E4M3)

        def y1_product(n, cols, b, stage):
            bank = take_bank(b, cols.stop - cols.start)
            nc.tensor.matmul_mx(
                out=bank[:],
                lhsT=w3_w[:, 2 * P * n : 2 * P * (n + 1)].bitcast(E2M1),
                lhsT_scale=w3_s[:, P * n : P * (n + 1)],
                rhs=z1_codes(cols),
                rhs_scale=z1_s[:, cols],
                start=True,
                stop=True,
            )
            nc.scalar.copy(stage, bank[:])

        def scatter(n, offsets, values, weights):
            nc.vector.tensor_tensor(pages[n][:].indirect(offsets), values, weights, ALU.mult)

        banks = []

        def keep_h1(b):
            nc.scalar.copy(h1[:, :, P * b : P * (b + 1)], banks[b][:])

        def stage_first(c, over=None):
            first[c.start] = held([P, c.stop - c.start], F32, "y1_0_%d" % c.start, over)
            y1_product(0, c, 7, first[c.start][:])

        def scatter_first(c):
            scatter(0, offs3_t[:, c.start // 16 : c.stop // 16], first[c.start][:], wg1_t[:, c])

        for k, chunk in enumerate(chunks):
            z1_g = held([P, chunk.stop - chunk.start, PACK], BF16, "z1_g%d" % chunk.start, *(("w2_g_place", 3072) if chunk.stop == S else ()))
            for c in range(chunk.start, chunk.stop, P):
                cols = slice(c, c + P)
                if len(banks) == 2:
                    keep_h1(0)
                bank = take_bank(len(banks) % 7, PACK, P)
                for t in range(PACK):
                    nc.tensor.matmul_mx(
                        out=bank[:, t, :],
                        lhsT=w1_c[:, P * t : P * (t + 1)].bitcast(E4M3),
                        lhsT_scale=w1_s[:, P * t : P * (t + 1)],
                        rhs=v_w[:, cols].bitcast(E4M3),
                        rhs_scale=v_s[:, cols],
                        start=True,
                        stop=True,
                    )
                nc.scalar.activation(z1_g[:, c - chunk.start : c - chunk.start + P, :], bank[:].rearrange("p t j -> p j t"), ACT.Abs)
                banks.append(bank)
            if chunk.start == BANK:
                z1_c.append(held([P, BANK], U32, "z1_c1", "z1_g256", -1536))
            nc.vector.quantize_mx(
                out=z1_codes(chunk),
                scales=z1_s[:, chunk],
                in_=z1_g[:].rearrange("p c i -> p (c i)"),
            )
            if k == 1:
                stage_first(chunks[0], "z1_g256")
                v2_s = held([P, PM], U8, "v2_s", "z1_g256", 1536)
                nc.vector.tensor_copy(v2_s[:], tab2_s[:].indirect(offs2_t[:]))
            if k > 0:
                scatter_first(chunks[k - 1])
                stage_first(chunk)

        v2_w.append(gather_merchants(1, "w2_g_place", 4096))
        scatter_first(chunks[-1])

        def y1_tile(n, pair, over, skip=0):
            y1.append(held([P, S], F32, "y1_%d" % n, over, skip))
            for h in range(2):
                y1_product(n, slice(BANK * h, BANK * (h + 1)), pair[h], y1[n][:, BANK * h : BANK * (h + 1)])

        for b in range(1, len(banks)):
            keep_h1(b)

        w2_g = [held([P, H, PACK], BF16, "w2_g%d" % a, "w2_g_place", 6144 * a) for a in range(2)]
        w2_q = []
        for a in range(2):
            interleave(w2_g[a][:], w2_raw[a][:], 2)
            w2_q.append(quantize(w2_g[a][:], "w2_%d" % a))

        y1_tile(1, (7, 1), "w2_raw1")
        scatter(1, offs3_t[:], y1[1][:], wg1_t[:])
        pages.append(load_page(4))
        pages.append(load_page(5, "tab2_w1"))
        suspect = []
        for t, over in enumerate((None, None, "w2_g0", "w2_g1")):
            suspect.append(held([P, PM], F32, "suspect%d" % t, over))
            nc.vector.tensor_copy(suspect[t][:], h1[:, t, :].indirect(pos1_t[:]))
        y1_tile(2, (7, 1), "w2_raw1", 4096)

        turns = held([P, 4, H], F32, "turns")
        whole = held([P, 4, H], U32, "whole", "w1_raw0")
        minus = held([P, 4, H], F32, "minus")
        for jt in range(4):
            cols = slice(P * jt, P * (jt + 1))
            bank = take_bank((4, 5, 6, 0)[jt], BANK)
            for a in range(2):
                nc.tensor.matmul_mx(
                    out=bank[:],
                    lhsT=v2_w[a][:, cols].bitcast(E4M3),
                    lhsT_scale=v2_s[4 * a :, cols],
                    rhs=w2_q[a][0][:].bitcast(E4M3),
                    rhs_scale=w2_q[a][1][:],
                    start=(a == 0),
                    stop=(a == 1),
                )
            nc.scalar.activation(
                turns[:, jt, :].rearrange("p (t m) -> p t m", t=PACK),
                bank[:].rearrange("p (m t) -> p t m", t=PACK),
                ACT.Copy,
                scale=1.0 / (2.0 * math.pi),
            )
            nc.scalar.activation(whole[:, jt, :], turns[:, jt, :], ACT.Copy, bias=ROUNDER, scale=1.0)
            nc.scalar.activation(minus[:, jt, :], whole[:, jt, :], ACT.Copy, bias=ROUNDER, scale=-1.0)

        scatter(2, offs3_t[:], y1[2][:], wg1_t[:])
        y1_tile(3, (2, 3), "w2_raw0")
        scatter(3, offs3_t[:], y1[3][:], wg1_t[:])
        halves = [slice(0, BANK), slice(BANK, S)]
        y1_4 = [held([P, BANK], F32, "y1_4a", "w2_raw0", 4096)]
        y1_product(4, halves[0], 2, y1_4[0][:])
        scatter(4, offs3_t[:, :32], y1_4[0][:], wg1_t[:, halves[0]])
        y1.append(None)

        def add_turned(bank, first, second):
            for i, src in enumerate((first, second)):
                nc.tensor.matmul(bank, lhsT=src, rhs=ident[:], start=(i == 0), stop=(i == 1), is_transpose=True)

        sine = held([P, PACK, PM], F32, "sine")
        gained = held([P, PACK, PM], F32, "gained", "whole")
        for t in range(PACK):
            bank = take_bank((7, 1, 2, 3)[t], BANK)
            rows = slice(P * t, P * (t + 1))
            for jt in range(4):
                add_turned(bank[:, P * jt : P * (jt + 1)], turns[:, jt, rows], minus[:, jt, rows])
            nc.scalar.activation(sine[:, t, :], bank[:], ACT.Sin, scale=-2.0 * math.pi)
            nc.scalar.activation(gained[:, t, :], sine[:, t, :], ACT.Copy, scale=gain_t[:, t : t + 1])

        w4_g = held([P, N, PACK], BF16, "w4_g")
        interleave(w4_g[:], w4_raw[:], 4)
        w4_q = [quantize(w4_g[:, 384 * h : 384 * (h + 1), :], "w4_%d" % h) for h in range(2)]


        z2_t = held([P, 4, 2, P, 2], BF16, "z2_t", "sine", 2048)
        z2_g = held([P, PM, PACK], BF16, "z2_g")
        for jt in range(4):
            cols = slice(P * jt, P * (jt + 1))
            bank = take_bank((4, 5, 6, 0)[jt], PACK, P)
            for t in range(PACK):
                add_turned(bank[:, t, :], gained[:, t, cols], suspect[t][:, cols])
            nc.scalar.activation(
                z2_t[:, jt], bank[:].rearrange("j (u e) p -> j u p e", e=2), ACT.Copy, scale=-1.0
            )
        z2_t_words = z2_t[:].rearrange("j a u p e -> j a u (p e)").bitcast(F32)
        z2_g_words = z2_g[:].bitcast(F32).rearrange("p (a j) u -> p a j u", j=P)
        for h in range(2):
            bank = take_bank((7, 1)[h], 2, 2, P)
            for a in range(2):
                for u in range(2):
                    nc.tensor.transpose(bank[:, a, u, :], z2_t_words[:, 2 * h + a, u, :], ident[:])
            nc.scalar.copy(z2_g_words[:, 2 * h : 2 * h + 2], bank[:].rearrange("p a u j -> p a j u"))
        y1_4.append(held([P, BANK], F32, "y1_4b", "sine", 1024))
        y1_product(4, halves[1], 6, y1_4[1][:])
        y1_tile(5, (4, 5), "sine", 3072)

        minus_b, b_turned = [], []

        def direct(n):
            cols = slice(P * n, P * (n + 1))
            bank = take_bank(2 + n % 2, BANK)
            for a in range(2):
                nc.tensor.matmul_mx(
                    out=bank[:],
                    lhsT=w5_w[a][:, cols].bitcast(E4M3),
                    lhsT_scale=w5_s[4 * a :, cols],
                    rhs=v2_w[a][:].bitcast(E4M3),
                    rhs_scale=v2_s[4 * a :, :],
                    start=(a == 0),
                    stop=(a == 1),
                )
            over = ("tab2_w0", 2048 * n) if n < 4 else ("tab_w", 2048 * (n - 2))
            minus_b.append(held([P, PM], F32, "minus_b%d" % n, *over))
            nc.scalar.activation(minus_b[n][:], bank[:], ACT.Copy, scale=-1.0)
            bank = take_bank(4 + n % 2, 4, P)
            for jt in range(4):
                nc.tensor.transpose(bank[:, jt, :], minus_b[n][:, P * jt : P * (jt + 1)], ident[:])
            over = ("turns", 2048 * n) if n < 4 else ("minus", 2048 * (n - 4))
            b_turned.append(held([P, 4, P], F32, "b_turned%d" % n, *over))
            nc.scalar.activation(b_turned[n][:], bank[:], ACT.Copy, scale=-1.0)

        for n in range(2):
            direct(n)
        z2_c, z2_s = quantize(z2_g[:], "z2")
        scatter(4, offs3_t[:, 32:], y1_4[1][:], wg1_t[:, halves[1]])
        scatter(5, offs3_t[:], y1[5][:], wg1_t[:])

        def larger(n):
            cols = slice(P * (n % 3), P * (n % 3 + 1))
            bank = take_bank((6, 0)[n % 2], BANK)
            nc.tensor.matmul_mx(
                out=bank[:],
                lhsT=w4_q[n // 3][0][:, cols].bitcast(E4M3),
                lhsT_scale=w4_q[n // 3][1][:, cols],
                rhs=z2_c[:].bitcast(E4M3),
                rhs_scale=z2_s[:],
                start=True,
                stop=True,
            )
            a_sb = held([P, PM], F32, "a_sb%d" % n, "gained", 2048 * (n % 2))
            nc.scalar.copy(a_sb[:], bank[:])
            bank = take_bank((7, 1)[n % 2], 4, P)
            for jt in range(4):
                cols = slice(P * jt, P * (jt + 1))
                add_turned(bank[:, jt, :], a_sb[:, cols], minus_b[n][:, cols])
            excess = held([P, 4, P], F32, "excess%d" % n, "gained", 4096 + 2048 * (n % 2))
            nc.scalar.activation(excess[:], bank[:], ACT.Relu)
            bank = take_bank((7, 1)[n % 2], 4, P)
            for jt in range(4):
                add_turned(bank[:, jt, :], excess[:, jt, :], b_turned[n][:, jt, :])
            y2 = ring.tile([P, PM], F32, name="y2")
            nc.scalar.copy(y2[:], bank[:].rearrange("p a j -> p (a j)"))
            return y2

        for n in range(N_TILES):
            y2 = larger(n)
            scatter(n, offs4_t[:], y2[:], wg2_t[:])
            nc.sync.dma_start(out[P * n : P * (n + 1), :], pages[n][:])
            if n + 2 < N_TILES:
                direct(n + 2)
